import numpy as np
import ml_dtypes


def mxq(x, axis, fmt="e4m3"):
    dtype, down = {"e4m3": (ml_dtypes.float8_e4m3fn, 7), "e5m2": (ml_dtypes.float8_e5m2, 14)}[fmt]
    v = np.moveaxis(np.asarray(x, np.float32).astype(ml_dtypes.bfloat16).astype(np.float64), axis, -1)
    blocks = v.reshape(v.shape[:-1] + (-1, 32))
    amax = np.abs(blocks).max(-1, keepdims=True)
    byte = np.maximum(np.where(amax > 0, np.frexp(amax)[1] - 1 + 127, 0) - down, 1)
    scale = np.exp2(byte - 127.0)
    codes = (blocks / scale).astype(np.float32).astype(dtype).astype(np.float64)
    return np.moveaxis((codes * scale).reshape(v.shape), -1, axis)


WIDE = False


def mx_kscale(k):
    if not WIDE:
        return np.ones(k)
    levels = np.array([10, -10, 5, -5, 0])
    if k % 512:
        return np.exp2(np.random.permutation(np.resize(levels, k // 32))).repeat(32)
    a = np.empty((k // 512, 16))
    for p in range(k // 512):
        a[p, :8] = np.random.permutation(np.resize(levels, 8))
        for g in range(8):
            far = levels[np.abs(levels - a[p, g]) >= 10]
            a[p, g + 8] = far[np.random.randint(len(far))]
    return np.exp2(a.ravel()).repeat(32)


def f64(x):
    return np.asarray(x).astype(np.float64)


def striped(idx):
    return np.tile(idx.reshape(-1, 16).T, (8, 1)).astype(np.uint16)


def unstriped(offs):
    return offs[:16].T.reshape(-1).astype(np.int64)


def pack_weight(w):
    k, n = w.shape
    w = f64(np.asarray(w, np.float32).astype(ml_dtypes.bfloat16)).reshape(k // 32, 32, n)
    amax = np.abs(w).max(1)
    byte = np.clip(np.where(amax > 0, np.frexp(amax)[1] - 1 + 127 - 7, 1), 1, 254)
    scaled = (w * np.exp2(127.0 - byte)[:, None, :]).reshape(k, n).astype(np.float32)
    words = np.ascontiguousarray(scaled.reshape(k // 512, 128, 4, n).transpose(0, 1, 3, 2)).astype(ml_dtypes.float8_e4m3fn).view(np.uint8)
    return words, np.ascontiguousarray(byte.astype(np.uint8).reshape(k // 512, 16, n))


def unpack_weight(words, scales):
    g, p, n, _ = words.shape
    vals = np.ascontiguousarray(words).view(ml_dtypes.float8_e4m3fn).astype(np.float64) * np.repeat(np.exp2(scales.astype(np.float64) - 127.0), 8, axis=1)[..., None]
    return vals.transpose(0, 1, 3, 2).reshape(g * 512, n)


def relu(v):
    return np.maximum(v, 0.0)


K, T, S, D, N, H = 512, 2048, 1024, 4, 256, 512


def setup_inputs():
    n = np.random.standard_normal
    s = mx_kscale(K)[:, None]
    u = mx_kscale(H)
    packed_xT = pack_weight(n((K, T)) * s)
    return {
        "x_words": packed_xT[0],
        "x_scales": packed_xT[1],
        "w1": (n((K, H)) / np.sqrt(K) / s).astype(np.float32),
        "w2": (n((K, H)) / np.sqrt(K) / s).astype(np.float32),
        "lodf": (np.random.uniform(-0.6, 0.6, (H, S))).astype(np.float32),
        "unit": (np.random.uniform(0.6, 1.4, (H, 1)) * u[:, None]).astype(np.float32),
        "w3": (n((H, N)) / np.sqrt(H) / u[:, None]).astype(np.float32),
        "offs": striped(np.random.permutation(T)[:S]),
        "out_l": striped(np.random.permutation(S)),
    }


def reference(x_words, x_scales, w1, w2, lodf, unit, w3, offs, out_l):
    xq = unpack_weight(x_words, x_scales)[:, unstriped(offs)]
    fl = mxq(f64(w1), 0, "e4m3").T @ xq
    fo = fl[:, unstriped(out_l)]
    post = fl + fo * f64(lodf)
    lm = mxq(f64(w2), 0, "e4m3").T @ xq
    cap = np.log(np.exp(lm) + 1.0) + 0.5
    over = relu(np.abs(post) - cap)
    worst = over.reshape(len(over), -1, D).max(axis=2)
    hid = f64(unit) * (over + 0.5 * np.repeat(worst, D, axis=1) - (0.3 * post))
    return mxq(f64(w3), 0, "e4m3").T @ mxq(hid, 0, "e4m3")

@@ -1,0 +1,284 @@
+import math
+from contextlib import ExitStack
+
+import concourse.mybir as mybir
+from concourse.masks import make_identity
+
+K, T, S, D, N, H = 512, 2048, 1024, 4, 256, 512
+FLOPS = 2 * K * H * S * 2 + 2 * H * N * S
+
+F32 = mybir.dt.float32
+BF16 = mybir.dt.bfloat16
+I32 = mybir.dt.int32
+U32 = mybir.dt.uint32
+U16 = mybir.dt.uint16
+U8 = mybir.dt.uint8
+FP8X4 = mybir.dt.float8_e4m3fn_x4
+ALU = mybir.AluOpType
+ACT = mybir.ActivationFunctionType
+
+P = 128
+PACK = 4
+HALF = 512
+BLOCK = 128
+CHUNK = 256
+HALVES = S // HALF
+BLOCKS = S // BLOCK
+FLOW = 0.3
+TINY = 2.0 ** -60
+
+
+def tile_picked_ylopfw_risk_p_kernel(
+    tc, x_words, x_scales, w1, w2, lodf, unit, w3, offs, out_l, out
+):
+    nc = tc.nc
+    with ExitStack() as ctx:
+        keep = ctx.enter_context(tc.tile_pool(name="keep", bufs=1))
+        ring = ctx.enter_context(tc.tile_pool(name="ring", bufs=3))
+        psum = ctx.enter_context(tc.psum_pool(name="psum", bufs=1))
+
+        def bank(number, name):
+            return psum.tile([P, 512], F32, name=name, tag="bank%d" % number)
+
+        def quantize(values, width, name):
+            codes = keep.tile([P, width], U32, name=name + "_codes", align_bytes=64)
+            scales = keep.tile([P, width], U8, name=name + "_scales", align_bytes=64)
+            nc.vector.quantize_mx(out=codes[:].bitcast(FP8X4), scales=scales[:], in_=values)
+            return codes, scales
+
+        def product(acc, stationary, s_cols, moving, m_cols):
+            nc.tensor.matmul_mx(
+                out=acc,
+                lhsT=stationary[0][:, s_cols].bitcast(FP8X4),
+                lhsT_scale=stationary[1][:, s_cols],
+                rhs=moving[0][:, m_cols].bitcast(FP8X4),
+                rhs_scale=moving[1][:, m_cols],
+                start=True,
+                stop=True,
+            )
+
+        offs_t = keep.tile([P, S // 16], U16, name="offs_t")
+        nc.sync.dma_start(offs_t[:], offs)
+        table_scales = keep.tile([P, T], U8, name="table_scales", align_bytes=64)
+        nc.vector.memset(table_scales[:].bitcast(I32), 0)
+        for q in range(4):
+            nc.scalar.dma_start(
+                table_scales[32 * q : 32 * q + 4, :].bitcast(I32),
+                x_scales[0, 4 * q : 4 * q + 4, :].bitcast(I32),
+            )
+        table_words = keep.tile([P, T], I32, name="table_words", align_bytes=64)
+        nc.sync.dma_start(table_words[:], x_words[0].rearrange("p n t -> p (n t)").bitcast(I32))
+        w1_rows = w1.rearrange("(p j) c -> p j c", j=PACK)
+        w1_raw = []
+        for half in range(2):
+            raw = keep.tile([P, PACK, H // 2], F32, name="w1_raw%d" % half)
+            nc.sync.dma_start(raw[:], w1_rows[:, :, half * (H // 2) : (half + 1) * (H // 2)])
+            w1_raw.append(raw)
+        outl_t = keep.tile([P, S // 16], U16, name="outl_t")
+        nc.sync.dma_start(outl_t[:], out_l)
+        lodf_rows = lodf.rearrange("(p t) j -> p t j", t=PACK)
+        factors = []
+        for t in range(PACK):
+            factor = keep.tile([P, S], F32, name="factor%d" % t)
+            factors.append(factor)
+        nc.sync.dma_start(factors[0][:], lodf_rows[:, 0, :])
+        w2_raw = keep.tile([P, PACK, H], F32, name="w2_raw")
+        nc.sync.dma_start(w2_raw[:], w2.rearrange("(p j) c -> p j c", j=PACK))
+        for t in range(1, PACK):
+            nc.sync.dma_start(factors[t][:], lodf_rows[:, t, :])
+        w3_raw = keep.tile([P, PACK, N], F32, name="w3_raw")
+        nc.sync.dma_start(w3_raw[:], w3.rearrange("(p j) c -> p j c", j=PACK))
+        unit_t = keep.tile([P, PACK], F32, name="unit_t")
+        nc.sync.dma_start(unit_t[:], unit.rearrange("(p t) o -> p (t o)", t=PACK))
+        identity = keep.tile([P, P], F32, name="identity")
+        make_identity(nc, identity[:])
+
+        picked = []
+        for half in range(HALVES):
+            entries = offs_t[:, half * (HALF // 16) : (half + 1) * (HALF // 16)]
+            words = keep.tile([P, HALF], U32, name="picked_words%d" % half, align_bytes=64)
+            nc.vector.tensor_copy(words[:], table_words[:].bitcast(U32).indirect(entries))
+            picked.append([words])
+        for half in range(HALVES):
+            entries = offs_t[:, half * (HALF // 16) : (half + 1) * (HALF // 16)]
+            scales = keep.tile([P, HALF], U8, name="picked_scales%d" % half, align_bytes=64)
+            nc.vector.tensor_copy(scales[:], table_scales[:].indirect(entries))
+            picked[half].append(scales)
+
+        w1_bf = keep.tile([P, PACK, P, PACK], BF16, name="w1_bf", align_bytes=64)
+        for half in range(2):
+            nc.scalar.copy(
+                w1_bf[:, :, half * 64 : (half + 1) * 64, :].rearrange("p t m j -> p m t j"),
+                w1_raw[half][:].rearrange("p j (m t) -> p m t j", t=PACK),
+            )
+        w1_q = quantize(w1_bf[:].rearrange("p t m j -> p (t m j)"), H, "w1")
+
+        flows = []
+        for t in range(PACK):
+            flow = keep.tile([P, S], F32, name="flow%d" % t)
+            flows.append(flow)
+        posts = []
+        for half in range(HALVES):
+            post = keep.tile([P, PACK, HALF], F32, name="post%d" % half)
+            posts.append(post)
+
+        def flow_tile(t):
+            for half in range(HALVES):
+                acc = bank(half, "flow_acc")
+                product(acc[:], w1_q, slice(t * P, (t + 1) * P), picked[half], slice(0, HALF))
+                nc.scalar.activation(
+                    flows[t][:, half * HALF : (half + 1) * HALF], acc[:], ACT.Copy, scale=-FLOW
+                )
+
+        def post_tile(t, half):
+            cols = slice(half * HALF, (half + 1) * HALF)
+            entries = outl_t[:, half * (HALF // 16) : (half + 1) * (HALF // 16)]
+            other = ring.tile([P, HALF], F32, name="other")
+            nc.vector.tensor_tensor(other[:], flows[t][:].indirect(entries), factors[t][:, cols], ALU.mult)
+            return lambda: nc.vector.tensor_tensor(posts[half][:, t, :], other[:], flows[t][:, cols], ALU.add)
+
+        for t in range(3):
+            flow_tile(t)
+        w2_bf = keep.tile([P, H, PACK], BF16, name="w2_bf", align_bytes=64)
+        nc.scalar.activation(
+            w2_bf[:], w2_raw[:].rearrange("p j c -> p c j"), ACT.Copy, scale=-1.0
+        )
+        flow_tile(3)
+        pending = post_tile(0, 0)
+        for t in range(1, 3):
+            following = post_tile(t, 0)
+            pending()
+            pending = following
+        w2_q = quantize(w2_bf[:].rearrange("p c j -> p (c j)"), H, "w2")
+        following = post_tile(3, 0)
+        pending()
+        pending = following
+
+        stage = keep.tile([P, BLOCKS + 1, H], F32, name="stage")
+        limit_acc = {}
+        for b in list(range(1, BLOCKS)) + [0]:
+            half, c = divmod(b, HALF // BLOCK)
+            acc = bank((b + 1) % BLOCKS, "limit_acc")
+            product(acc[:], picked[half], slice(c * BLOCK, (c + 1) * BLOCK), w2_q, slice(0, H))
+            limit_acc[b] = acc[:].rearrange("j (m t) -> j t m", t=PACK)
+            nc.scalar.activation(
+                stage[:, b + 1, :].rearrange("j (t m) -> j t m", t=PACK), limit_acc[b], ACT.Sigmoid
+            )
+        for t in range(PACK):
+            following = post_tile(t, 1)
+            pending()
+            pending = following
+        pending()
+
+        w3_bf = keep.tile([P, N, PACK], BF16, name="w3_bf", align_bytes=64)
+        half_unit = keep.tile([P, PACK], F32, name="half_unit")
+        nc.vector.tensor_scalar(half_unit[:], unit_t[:], 0.5, None, ALU.mult)
+
+        neg_caps = []
+        for b in range(BLOCKS):
+            nc.scalar.activation(
+                stage[:, b, :], stage[:, b + 1, :], ACT.Ln, bias=TINY, scale=math.exp(-0.5)
+            )
+        nc.scalar.copy(w3_bf[:], w3_raw[:].rearrange("p j c -> p c j"))
+
+        def neg_cap(b):
+            cap = keep.tile([P, H], F32, name="neg_cap%d" % b)
+            nc.vector.scalar_tensor_tensor(
+                cap[:].rearrange("j (t m) -> j t m", t=PACK),
+                limit_acc[b],
+                -0.5,
+                stage[:, b, :].rearrange("j (t m) -> j t m", t=PACK),
+                ALU.add,
+                ALU.min,
+            )
+            neg_caps.append(cap)
+
+        def excess(b):
+            half, c = divmod(b, HALF // BLOCK)
+            turned = bank((1, 3, 5)[b % 3], "turned")
+            for t in range(PACK):
+                nc.tensor.transpose(
+                    turned[:, t * P : (t + 1) * P],
+                    posts[half][:, t, c * BLOCK : (c + 1) * BLOCK],
+                    identity[:],
+                )
+            size = ring.tile([P, H], F32, name="size")
+            nc.scalar.activation(size[:], turned[:], ACT.Abs, scale=1.0 / FLOW)
+            gap = bank((2, 4, 6)[b % 3], "gap")
+            for t in range(PACK):
+                cols = slice(t * P, (t + 1) * P)
+                nc.tensor.matmul(gap[:, cols], size[:, cols], identity[:], start=True, stop=False, is_transpose=True)
+                nc.tensor.matmul(gap[:, cols], neg_caps[b][:, cols], identity[:], start=False, stop=True, is_transpose=True)
+            return gap
+
+        def fold(b, gap, largest, mixed):
+            half, c = divmod(b, HALF // BLOCK)
+            e = b % (CHUNK // BLOCK)
+            groups = BLOCK // D
+            nc.vector.tensor_reduce(
+                largest[:, :, e * groups : (e + 1) * groups],
+                gap[:].rearrange("p (t v d) -> p t v d", t=PACK, d=D),
+                mybir.AxisListType.X,
+                ALU.max,
+            )
+            nc.vector.scalar_tensor_tensor(
+                mixed[:, :, e * BLOCK : (e + 1) * BLOCK],
+                gap[:].rearrange("p (t j) -> p t j", t=PACK),
+                0.0,
+                posts[half][:, :, c * BLOCK : (c + 1) * BLOCK],
+                ALU.max,
+                ALU.add,
+            )
+
+        def hidden(largest, mixed):
+            groups = CHUNK // D
+            share = ring.tile([P, PACK, groups], F32, name="share")
+            nc.vector.scalar_tensor_tensor(
+                share[:], largest[:], 0.0,
+                half_unit[:].unsqueeze(2).to_broadcast([P, PACK, groups]),
+                ALU.max, ALU.mult,
+            )
+            hid = ring.tile([P, PACK, CHUNK], BF16, name="hid")
+            for t in range(PACK):
+                nc.vector.scalar_tensor_tensor(
+                    hid[:, t, :].rearrange("p (v d) -> p v d", d=D),
+                    mixed[:, t, :].rearrange("p (v d) -> p v d", d=D),
+                    unit_t[:, t : t + 1],
+                    share[:, t, :].unsqueeze(2).to_broadcast([P, groups, D]),
+                    ALU.mult,
+                    ALU.add,
+                )
+            woven = ring.tile([P, CHUNK, PACK], BF16, name="woven", align_bytes=64)
+            nc.scalar.copy(woven[:], hid[:].rearrange("p t j -> p j t"))
+            return woven
+
+        out_rows = out.rearrange("(g p) j -> p g j", p=P)
+
+        def finish(chunk, woven):
+            hid_q = quantize(woven[:].rearrange("p j t -> p (j t)"), CHUNK, "hid%d" % chunk)
+            acc = bank((7, 0)[chunk % 2], "out_acc")
+            for g in range(N // P):
+                product(acc[:, g * CHUNK : (g + 1) * CHUNK], w3_q, slice(g * P, (g + 1) * P), hid_q, slice(0, CHUNK))
+            result = ring.tile([P, N // P, CHUNK], F32, name="result")
+            nc.scalar.copy(result[:], acc[:].rearrange("p (g j) -> p g j", j=CHUNK))
+            nc.sync.dma_start(out_rows[:, :, chunk * CHUNK : (chunk + 1) * CHUNK], result[:])
+
+        for b in range(4):
+            neg_cap(b)
+        gaps = {0: excess(0), 1: excess(1)}
+        w3_q = quantize(w3_bf[:].rearrange("p c j -> p (c j)"), N, "w3")
+        waiting = None
+        for chunk in range(S // CHUNK):
+            largest = ring.tile([P, PACK, CHUNK // D], F32, name="largest")
+            mixed = ring.tile([P, PACK, CHUNK], F32, name="mixed")
+            for b in (2 * chunk, 2 * chunk + 1):
+                for ahead in (4 + 2 * b, 5 + 2 * b):
+                    if ahead < BLOCKS:
+                        neg_cap(ahead)
+                if b + 2 < BLOCKS:
+                    gaps[b + 2] = excess(b + 2)
+                fold(b, gaps[b], largest, mixed)
+            if waiting is not None:
+                finish(chunk - 1, waiting)
+            waiting = hidden(largest, mixed)
+        finish(S // CHUNK - 1, waiting)

@@ -21,7 +21,7 @@ P = 128
 PACK = 4
 HALF = 512
 BLOCK = 128
-CHUNK = 256
+CHUNKS = ((0, 1), (2, 3), (4, 5), (6,), (7,))
 HALVES = S // HALF
 BLOCKS = S // BLOCK
 FLOW = 0.3
@@ -60,32 +60,35 @@ def tile_picked_ylopfw_risk_p_kernel(
         offs_t = keep.tile([P, S // 16], U16, name="offs_t")
         nc.sync.dma_start(offs_t[:], offs)
         table_scales = keep.tile([P, T], U8, name="table_scales", align_bytes=64)
-        nc.vector.memset(table_scales[:].bitcast(I32), 0)
+        nc.gpsimd.memset(table_scales[:].bitcast(I32), 0)
         for q in range(4):
-            nc.scalar.dma_start(
+            nc.sync.dma_start(
                 table_scales[32 * q : 32 * q + 4, :].bitcast(I32),
                 x_scales[0, 4 * q : 4 * q + 4, :].bitcast(I32),
             )
-        table_words = keep.tile([P, T], I32, name="table_words", align_bytes=64)
-        nc.sync.dma_start(table_words[:], x_words[0].rearrange("p n t -> p (n t)").bitcast(I32))
         w1_rows = w1.rearrange("(p j) c -> p j c", j=PACK)
         w1_raw = []
         for half in range(2):
             raw = keep.tile([P, PACK, H // 2], F32, name="w1_raw%d" % half)
             nc.sync.dma_start(raw[:], w1_rows[:, :, half * (H // 2) : (half + 1) * (H // 2)])
             w1_raw.append(raw)
+        table_words = keep.tile([P, T], I32, name="table_words", align_bytes=64)
+        nc.sync.dma_start(table_words[:], x_words[0].rearrange("p n t -> p (n t)").bitcast(I32))
         outl_t = keep.tile([P, S // 16], U16, name="outl_t")
         nc.sync.dma_start(outl_t[:], out_l)
         lodf_rows = lodf.rearrange("(p t) j -> p t j", t=PACK)
-        factors = []
-        for t in range(PACK):
-            factor = keep.tile([P, S], F32, name="factor%d" % t)
-            factors.append(factor)
-        nc.sync.dma_start(factors[0][:], lodf_rows[:, 0, :])
+        factors = {}
+
+        def load_factors(t, half):
+            factor = keep.tile([P, HALF], F32, name="factor%d_%d" % (t, half))
+            nc.sync.dma_start(factor[:], lodf_rows[:, t, half * HALF : (half + 1) * HALF])
+            factors[t, half] = factor
+
         w2_raw = keep.tile([P, PACK, H], F32, name="w2_raw")
         nc.sync.dma_start(w2_raw[:], w2.rearrange("(p j) c -> p j c", j=PACK))
-        for t in range(1, PACK):
-            nc.sync.dma_start(factors[t][:], lodf_rows[:, t, :])
+        for half in range(HALVES):
+            for t in range(PACK):
+                load_factors(t, half)
         w3_raw = keep.tile([P, PACK, N], F32, name="w3_raw")
         nc.sync.dma_start(w3_raw[:], w3.rearrange("(p j) c -> p j c", j=PACK))
         unit_t = keep.tile([P, PACK], F32, name="unit_t")
@@ -93,19 +96,21 @@ def tile_picked_ylopfw_risk_p_kernel(
         identity = keep.tile([P, P], F32, name="identity")
         make_identity(nc, identity[:])
 
+        warm = keep.tile([P, 1], F32, name="warm")
+        nc.scalar.activation(warm[:], identity[:, 0:1], ACT.Sigmoid)
         picked = []
-        for half in range(HALVES):
-            entries = offs_t[:, half * (HALF // 16) : (half + 1) * (HALF // 16)]
-            words = keep.tile([P, HALF], U32, name="picked_words%d" % half, align_bytes=64)
-            nc.vector.tensor_copy(words[:], table_words[:].bitcast(U32).indirect(entries))
-            picked.append([words])
         for half in range(HALVES):
             entries = offs_t[:, half * (HALF // 16) : (half + 1) * (HALF // 16)]
             scales = keep.tile([P, HALF], U8, name="picked_scales%d" % half, align_bytes=64)
             nc.vector.tensor_copy(scales[:], table_scales[:].indirect(entries))
-            picked[half].append(scales)
+            picked.append([scales])
+        for half in range(HALVES):
+            entries = offs_t[:, half * (HALF // 16) : (half + 1) * (HALF // 16)]
+            words = keep.tile([P, HALF], U32, name="picked_words%d" % half, align_bytes=64)
+            nc.vector.tensor_copy(words[:], table_words[:].bitcast(U32).indirect(entries))
+            picked[half] = [words] + picked[half]
 
-        w1_bf = keep.tile([P, PACK, P, PACK], BF16, name="w1_bf", align_bytes=64)
+        w1_bf = keep.tile([P, PACK, P, PACK], BF16, name="w1_bf", tag="w_bf", align_bytes=64)
         for half in range(2):
             nc.scalar.copy(
                 w1_bf[:, :, half * 64 : (half + 1) * 64, :].rearrange("p t m j -> p m t j"),
@@ -117,69 +122,67 @@ def tile_picked_ylopfw_risk_p_kernel(
         for t in range(PACK):
             flow = keep.tile([P, S], F32, name="flow%d" % t)
             flows.append(flow)
-        posts = []
-        for half in range(HALVES):
-            post = keep.tile([P, PACK, HALF], F32, name="post%d" % half)
-            posts.append(post)
+        posts = [keep.tile([P, PACK, HALF], F32, name="post0")]
 
         def flow_tile(t):
             for half in range(HALVES):
-                acc = bank(half, "flow_acc")
+                acc = bank((2 * t + half) % 4, "flow_acc")
                 product(acc[:], w1_q, slice(t * P, (t + 1) * P), picked[half], slice(0, HALF))
                 nc.scalar.activation(
                     flows[t][:, half * HALF : (half + 1) * HALF], acc[:], ACT.Copy, scale=-FLOW
                 )
 
-        def post_tile(t, half):
-            cols = slice(half * HALF, (half + 1) * HALF)
+        def fetch(t, half, other):
             entries = outl_t[:, half * (HALF // 16) : (half + 1) * (HALF // 16)]
-            other = ring.tile([P, HALF], F32, name="other")
-            nc.vector.tensor_tensor(other[:], flows[t][:].indirect(entries), factors[t][:, cols], ALU.mult)
-            return lambda: nc.vector.tensor_tensor(posts[half][:, t, :], other[:], flows[t][:, cols], ALU.add)
+            nc.vector.tensor_tensor(other, flows[t][:].indirect(entries), factors[t, half][:], ALU.mult)
 
-        for t in range(3):
-            flow_tile(t)
-        w2_bf = keep.tile([P, H, PACK], BF16, name="w2_bf", align_bytes=64)
-        nc.scalar.activation(
-            w2_bf[:], w2_raw[:].rearrange("p j c -> p c j"), ACT.Copy, scale=-1.0
+        w2_bf = keep.tile([P, H, PACK], BF16, name="w2_bf", tag="w_bf", align_bytes=64)
+        nc.vector.tensor_scalar(
+            w2_bf[:].rearrange("p (c i) j -> p c j i", i=4),
+            w2_raw[:].rearrange("p j (c i) -> p c j i", i=4),
+            -1.0, None, ALU.mult,
         )
-        flow_tile(3)
-        pending = post_tile(0, 0)
-        for t in range(1, 3):
-            following = post_tile(t, 0)
-            pending()
-            pending = following
         w2_q = quantize(w2_bf[:].rearrange("p c j -> p (c j)"), H, "w2")
-        following = post_tile(3, 0)
-        pending()
-        pending = following
+        for t in range(PACK):
+            flow_tile(t)
+        others = {}
+        for half, t in [(0, 0), (0, 1), (0, 2), (0, 3), (1, 0), (1, 1)]:
+            others[t, half] = keep.tile([P, HALF], F32, name="other%d_%d" % (t, half))
+            fetch(t, half, others[t, half][:])
+            if half == 0:
+                nc.vector.tensor_tensor(posts[0][:, t, :], others[t, 0][:], flows[t][:, :HALF], ALU.add)
 
-        stage = keep.tile([P, BLOCKS + 1, H], F32, name="stage")
+        w3_bf = keep.tile([P, N, PACK], BF16, name="w3_bf", align_bytes=64)
+        nc.vector.tensor_copy(
+            w3_bf[:].rearrange("p (c i) j -> p c j i", i=4),
+            w3_raw[:].rearrange("p j (c i) -> p c j i", i=4),
+        )
+
+        w3_q = quantize(w3_bf[:].rearrange("p c j -> p (c j)"), N, "w3")
+        def stage(slot, shape, dtype, name):
+            return keep.tile(shape, dtype, name=name, tag="stage%d" % slot, align_bytes=64)
+
+        PAIRS = BLOCKS // 2
+        squashed = [stage(k + 1, [P, 2, H], F32, "squashed") for k in range(PAIRS)]
         limit_acc = {}
-        for b in list(range(1, BLOCKS)) + [0]:
+        for b in [4, 5, 6, 7, 2, 3, 0, 1]:
             half, c = divmod(b, HALF // BLOCK)
-            acc = bank((b + 1) % BLOCKS, "limit_acc")
+            acc = bank(b, "limit_acc")
             product(acc[:], picked[half], slice(c * BLOCK, (c + 1) * BLOCK), w2_q, slice(0, H))
             limit_acc[b] = acc[:].rearrange("j (m t) -> j t m", t=PACK)
             nc.scalar.activation(
-                stage[:, b + 1, :].rearrange("j (t m) -> j t m", t=PACK), limit_acc[b], ACT.Sigmoid
+                squashed[b // 2][:, b % 2, :].rearrange("j (t m) -> j t m", t=PACK), limit_acc[b], ACT.Sigmoid
             )
-        for t in range(PACK):
-            following = post_tile(t, 1)
-            pending()
-            pending = following
-        pending()
 
-        w3_bf = keep.tile([P, N, PACK], BF16, name="w3_bf", align_bytes=64)
         half_unit = keep.tile([P, PACK], F32, name="half_unit")
         nc.vector.tensor_scalar(half_unit[:], unit_t[:], 0.5, None, ALU.mult)
 
         neg_caps = []
-        for b in range(BLOCKS):
-            nc.scalar.activation(
-                stage[:, b, :], stage[:, b + 1, :], ACT.Ln, bias=TINY, scale=math.exp(-0.5)
-            )
-        nc.scalar.copy(w3_bf[:], w3_raw[:].rearrange("p j c -> p c j"))
+        logs = []
+        for k in range(PAIRS):
+            logged = stage(k, [P, 2, H], F32, "logged")
+            nc.scalar.activation(logged[:], squashed[k][:], ACT.Ln, bias=TINY, scale=math.exp(-0.5))
+            logs.append(logged)
 
         def neg_cap(b):
             cap = keep.tile([P, H], F32, name="neg_cap%d" % b)
@@ -187,7 +190,7 @@ def tile_picked_ylopfw_risk_p_kernel(
                 cap[:].rearrange("j (t m) -> j t m", t=PACK),
                 limit_acc[b],
                 -0.5,
-                stage[:, b, :].rearrange("j (t m) -> j t m", t=PACK),
+                logs[b // 2][:, b % 2, :].rearrange("j (t m) -> j t m", t=PACK),
                 ALU.add,
                 ALU.min,
             )
@@ -195,7 +198,7 @@ def tile_picked_ylopfw_risk_p_kernel(
 
         def excess(b):
             half, c = divmod(b, HALF // BLOCK)
-            turned = bank((1, 3, 5)[b % 3], "turned")
+            turned = bank((0, 2, 4)[b % 3], "turned")
             for t in range(PACK):
                 nc.tensor.transpose(
                     turned[:, t * P : (t + 1) * P],
@@ -204,16 +207,15 @@ def tile_picked_ylopfw_risk_p_kernel(
                 )
             size = ring.tile([P, H], F32, name="size")
             nc.scalar.activation(size[:], turned[:], ACT.Abs, scale=1.0 / FLOW)
-            gap = bank((2, 4, 6)[b % 3], "gap")
+            gap = bank((1, 3, 5)[b % 3], "gap")
             for t in range(PACK):
                 cols = slice(t * P, (t + 1) * P)
                 nc.tensor.matmul(gap[:, cols], size[:, cols], identity[:], start=True, stop=False, is_transpose=True)
                 nc.tensor.matmul(gap[:, cols], neg_caps[b][:, cols], identity[:], start=False, stop=True, is_transpose=True)
             return gap
 
-        def fold(b, gap, largest, mixed):
+        def fold(b, e, gap, largest, mixed):
             half, c = divmod(b, HALF // BLOCK)
-            e = b % (CHUNK // BLOCK)
             groups = BLOCK // D
             nc.vector.tensor_reduce(
                 largest[:, :, e * groups : (e + 1) * groups],
@@ -230,15 +232,15 @@ def tile_picked_ylopfw_risk_p_kernel(
                 ALU.add,
             )
 
-        def hidden(largest, mixed):
-            groups = CHUNK // D
+        def hidden(width, largest, mixed, weave):
+            groups = width // D
             share = ring.tile([P, PACK, groups], F32, name="share")
             nc.vector.scalar_tensor_tensor(
                 share[:], largest[:], 0.0,
                 half_unit[:].unsqueeze(2).to_broadcast([P, PACK, groups]),
                 ALU.max, ALU.mult,
             )
-            hid = ring.tile([P, PACK, CHUNK], BF16, name="hid")
+            hid = ring.tile([P, PACK, width], BF16, name="hid")
             for t in range(PACK):
                 nc.vector.scalar_tensor_tensor(
                     hid[:, t, :].rearrange("p (v d) -> p v d", d=D),
@@ -248,37 +250,46 @@ def tile_picked_ylopfw_risk_p_kernel(
                     ALU.mult,
                     ALU.add,
                 )
-            woven = ring.tile([P, CHUNK, PACK], BF16, name="woven", align_bytes=64)
-            nc.scalar.copy(woven[:], hid[:].rearrange("p t j -> p j t"))
+            woven = ring.tile([P, width, PACK], BF16, name="woven", align_bytes=64)
+            weave(
+                woven[:].rearrange("p (c i) t -> p c t i", i=4),
+                hid[:].rearrange("p t (c i) -> p c t i", i=4),
+            )
             return woven
 
         out_rows = out.rearrange("(g p) j -> p g j", p=P)
 
-        def finish(chunk, woven):
-            hid_q = quantize(woven[:].rearrange("p j t -> p (j t)"), CHUNK, "hid%d" % chunk)
-            acc = bank((7, 0)[chunk % 2], "out_acc")
+        def finish(chunk, first, width, woven):
+            hid_q = quantize(woven[:].rearrange("p j t -> p (j t)"), width, "hid%d" % chunk)
+            acc = bank((6, 7)[chunk % 2], "out_acc")
             for g in range(N // P):
-                product(acc[:, g * CHUNK : (g + 1) * CHUNK], w3_q, slice(g * P, (g + 1) * P), hid_q, slice(0, CHUNK))
-            result = ring.tile([P, N // P, CHUNK], F32, name="result")
-            nc.scalar.copy(result[:], acc[:].rearrange("p (g j) -> p g j", j=CHUNK))
-            nc.sync.dma_start(out_rows[:, :, chunk * CHUNK : (chunk + 1) * CHUNK], result[:])
+                product(acc[:, g * width : (g + 1) * width], w3_q, slice(g * P, (g + 1) * P), hid_q, slice(0, width))
+            result = ring.tile([P, N // P, width], F32, name="result")
+            nc.scalar.copy(result[:], acc[:, : (N // P) * width].rearrange("p (g j) -> p g j", j=width))
+            nc.sync.dma_start(out_rows[:, :, first : first + width], result[:])
 
-        for b in range(4):
+        for t in (2, 3):
+            neg_cap(2 * t - 4)
+            neg_cap(2 * t - 3)
+            others[t, 1] = stage(t - 2, [P, HALF], F32, "other_late")
+            fetch(t, 1, others[t, 1][:])
+        posts.append(keep.tile([P, PACK, HALF], F32, name="post1", tag="factor3_1"))
+        for t in range(PACK):
+            nc.gpsimd.tensor_tensor(posts[1][:, t, :], others[t, 1][:], flows[t][:, HALF:], ALU.add)
+        for b in range(4, BLOCKS):
             neg_cap(b)
         gaps = {0: excess(0), 1: excess(1)}
-        w3_q = quantize(w3_bf[:].rearrange("p c j -> p (c j)"), N, "w3")
         waiting = None
-        for chunk in range(S // CHUNK):
-            largest = ring.tile([P, PACK, CHUNK // D], F32, name="largest")
-            mixed = ring.tile([P, PACK, CHUNK], F32, name="mixed")
-            for b in (2 * chunk, 2 * chunk + 1):
-                for ahead in (4 + 2 * b, 5 + 2 * b):
-                    if ahead < BLOCKS:
-                        neg_cap(ahead)
+        for chunk, blocks in enumerate(CHUNKS):
+            width = len(blocks) * BLOCK
+            largest = ring.tile([P, PACK, width // D], F32, name="largest")
+            mixed = ring.tile([P, PACK, width], F32, name="mixed")
+            for e, b in enumerate(blocks):
                 if b + 2 < BLOCKS:
                     gaps[b + 2] = excess(b + 2)
-                fold(b, gaps[b], largest, mixed)
+                fold(b, e, gaps[b], largest, mixed)
             if waiting is not None:
-                finish(chunk - 1, waiting)
-            waiting = hidden(largest, mixed)
-        finish(S // CHUNK - 1, waiting)
+                finish(*waiting)
+            weave = nc.vector.tensor_copy if chunk == len(CHUNKS) - 1 else nc.scalar.copy
+            waiting = (chunk, blocks[0] * BLOCK, width, hidden(width, largest, mixed, weave))
+        finish(*waiting)

@@ -21,11 +21,21 @@ P = 128
 PACK = 4
 HALF = 512
 BLOCK = 128
-CHUNKS = ((0, 1), (2, 3), (4, 5), (6,), (7,))
+PAIR = 2 * BLOCK
 HALVES = S // HALF
 BLOCKS = S // BLOCK
-FLOW = 0.3
+PAIRS = S // PAIR
+LIST_ROW = 16
+RUN = 4
+PART = 0.3
 TINY = 2.0 ** -60
+
+HELD = 6
+PASSING = (6, 7)
+
+
+def held_bank(block):
+    return (block + 4) % HELD
 
 
 def tile_picked_ylopfw_risk_p_kernel(
@@ -38,7 +48,19 @@ def tile_picked_ylopfw_risk_p_kernel(
         psum = ctx.enter_context(tc.psum_pool(name="psum", bufs=1))
 
         def bank(number, name):
-            return psum.tile([P, 512], F32, name=name, tag="bank%d" % number)
+            return psum.tile([P, HALF], F32, name=name, tag="bank%d" % number)
+
+        def buffer(tag, shape, dtype, name):
+            return keep.tile(shape, dtype, name=name, tag=tag, align_bytes=64)
+
+        def entries(list_tile, half):
+            return list_tile[:, half * (HALF // LIST_ROW) : (half + 1) * (HALF // LIST_ROW)]
+
+        def weave_views(woven, rows):
+            return (
+                woven.rearrange("p (c i) j -> p c j i", i=RUN),
+                rows.rearrange("p j (c i) -> p c j i", i=RUN),
+            )
 
         def quantize(values, width, name):
             codes = keep.tile([P, width], U32, name=name + "_codes", align_bytes=64)
@@ -57,239 +79,279 @@ def tile_picked_ylopfw_risk_p_kernel(
                 stop=True,
             )
 
-        offs_t = keep.tile([P, S // 16], U16, name="offs_t")
+        def by_tile(view):
+            return view.rearrange("j (t m) -> j t m", t=PACK)
+
+        def drop_of(block):
+            half, place = divmod(block, HALF // BLOCK)
+            return drops[half][:, :, place * BLOCK : (place + 1) * BLOCK]
+
+        offs_t = keep.tile([P, S // LIST_ROW], U16, name="offs_t")
         nc.sync.dma_start(offs_t[:], offs)
         table_scales = keep.tile([P, T], U8, name="table_scales", align_bytes=64)
         nc.gpsimd.memset(table_scales[:].bitcast(I32), 0)
-        for q in range(4):
+        for quadrant in range(4):
             nc.sync.dma_start(
-                table_scales[32 * q : 32 * q + 4, :].bitcast(I32),
-                x_scales[0, 4 * q : 4 * q + 4, :].bitcast(I32),
+                table_scales[32 * quadrant : 32 * quadrant + 4, :].bitcast(I32),
+                x_scales[0, 4 * quadrant : 4 * quadrant + 4, :].bitcast(I32),
             )
         w1_rows = w1.rearrange("(p j) c -> p j c", j=PACK)
         w1_raw = []
-        for half in range(2):
-            raw = keep.tile([P, PACK, H // 2], F32, name="w1_raw%d" % half)
-            nc.sync.dma_start(raw[:], w1_rows[:, :, half * (H // 2) : (half + 1) * (H // 2)])
+        outl_t = keep.tile([P, S // LIST_ROW], U16, name="outl_t")
+        for side in range(2):
+            raw = keep.tile([P, PACK, H // 2], F32, name="w1_raw%d" % side)
+            nc.sync.dma_start(raw[:], w1_rows[:, :, side * (H // 2) : (side + 1) * (H // 2)])
             w1_raw.append(raw)
         table_words = keep.tile([P, T], I32, name="table_words", align_bytes=64)
         nc.sync.dma_start(table_words[:], x_words[0].rearrange("p n t -> p (n t)").bitcast(I32))
-        outl_t = keep.tile([P, S // 16], U16, name="outl_t")
         nc.sync.dma_start(outl_t[:], out_l)
+        w2_raw = buffer("w2_raw", [P, PACK, H], F32, "w2_raw")
+        nc.sync.dma_start(w2_raw[:], w2.rearrange("(p j) c -> p j c", j=PACK))
         lodf_rows = lodf.rearrange("(p t) j -> p t j", t=PACK)
         factors = {}
-
-        def load_factors(t, half):
-            factor = keep.tile([P, HALF], F32, name="factor%d_%d" % (t, half))
-            nc.sync.dma_start(factor[:], lodf_rows[:, t, half * HALF : (half + 1) * HALF])
-            factors[t, half] = factor
-
-        w2_raw = keep.tile([P, PACK, H], F32, name="w2_raw")
-        nc.sync.dma_start(w2_raw[:], w2.rearrange("(p j) c -> p j c", j=PACK))
         for half in range(HALVES):
             for t in range(PACK):
-                load_factors(t, half)
-        w3_raw = keep.tile([P, PACK, N], F32, name="w3_raw")
-        nc.sync.dma_start(w3_raw[:], w3.rearrange("(p j) c -> p j c", j=PACK))
+                factors[t, half] = keep.tile([P, HALF], F32, name="factor%d_%d" % (t, half))
+                nc.sync.dma_start(factors[t, half][:], lodf_rows[:, t, half * HALF : (half + 1) * HALF])
         unit_t = keep.tile([P, PACK], F32, name="unit_t")
         nc.sync.dma_start(unit_t[:], unit.rearrange("(p t) o -> p (t o)", t=PACK))
+        w3_raw = keep.tile([P, PACK, N], F32, name="w3_raw")
+        nc.sync.dma_start(w3_raw[:], w3.rearrange("(p j) c -> p j c", j=PACK))
         identity = keep.tile([P, P], F32, name="identity")
         make_identity(nc, identity[:])
 
         warm = keep.tile([P, 1], F32, name="warm")
         nc.scalar.activation(warm[:], identity[:, 0:1], ACT.Sigmoid)
+
+        picked_scales = []
+        for half in range(HALVES):
+            scales = keep.tile([P, HALF], U8, name="picked_scales%d" % half, align_bytes=64)
+            nc.vector.tensor_copy(scales[:], table_scales[:].indirect(entries(offs_t, half)))
+            picked_scales.append(scales)
         picked = []
         for half in range(HALVES):
-            entries = offs_t[:, half * (HALF // 16) : (half + 1) * (HALF // 16)]
-            scales = keep.tile([P, HALF], U8, name="picked_scales%d" % half, align_bytes=64)
-            nc.vector.tensor_copy(scales[:], table_scales[:].indirect(entries))
-            picked.append([scales])
-        for half in range(HALVES):
-            entries = offs_t[:, half * (HALF // 16) : (half + 1) * (HALF // 16)]
             words = keep.tile([P, HALF], U32, name="picked_words%d" % half, align_bytes=64)
-            nc.vector.tensor_copy(words[:], table_words[:].bitcast(U32).indirect(entries))
-            picked[half] = [words] + picked[half]
+            nc.vector.tensor_copy(words[:], table_words[:].bitcast(U32).indirect(entries(offs_t, half)))
+            picked.append((words, picked_scales[half]))
 
-        w1_bf = keep.tile([P, PACK, P, PACK], BF16, name="w1_bf", tag="w_bf", align_bytes=64)
-        for half in range(2):
+        w1_bf = buffer("w_bf", [P, PACK, P, PACK], BF16, "w1_bf")
+        for side in range(2):
             nc.scalar.copy(
-                w1_bf[:, :, half * 64 : (half + 1) * 64, :].rearrange("p t m j -> p m t j"),
-                w1_raw[half][:].rearrange("p j (m t) -> p m t j", t=PACK),
+                w1_bf[:, :, side * (P // 2) : (side + 1) * (P // 2), :].rearrange("p t m j -> p m t j"),
+                w1_raw[side][:].rearrange("p j (m t) -> p m t j", t=PACK),
             )
         w1_q = quantize(w1_bf[:].rearrange("p t m j -> p (t m j)"), H, "w1")
 
-        flows = []
-        for t in range(PACK):
-            flow = keep.tile([P, S], F32, name="flow%d" % t)
-            flows.append(flow)
-        posts = [keep.tile([P, PACK, HALF], F32, name="post0")]
+        flows = [keep.tile([P, S], F32, name="flow%d" % t) for t in range(PACK)]
+        drops = [keep.tile([P, PACK, HALF], F32, name="drop0")]
 
-        def flow_tile(t):
-            for half in range(HALVES):
-                acc = bank((2 * t + half) % 4, "flow_acc")
-                product(acc[:], w1_q, slice(t * P, (t + 1) * P), picked[half], slice(0, HALF))
-                nc.scalar.activation(
-                    flows[t][:, half * HALF : (half + 1) * HALF], acc[:], ACT.Copy, scale=-FLOW
-                )
-
-        def fetch(t, half, other):
-            entries = outl_t[:, half * (HALF // 16) : (half + 1) * (HALF // 16)]
-            nc.vector.tensor_tensor(other, flows[t][:].indirect(entries), factors[t, half][:], ALU.mult)
-
-        w2_bf = keep.tile([P, H, PACK], BF16, name="w2_bf", tag="w_bf", align_bytes=64)
-        nc.vector.tensor_scalar(
-            w2_bf[:].rearrange("p (c i) j -> p c j i", i=4),
-            w2_raw[:].rearrange("p j (c i) -> p c j i", i=4),
-            -1.0, None, ALU.mult,
-        )
+        w2_bf = buffer("w_bf", [P, H, PACK], BF16, "w2_bf")
+        nc.vector.tensor_scalar(*weave_views(w2_bf[:], w2_raw[:]), -1.0, None, ALU.mult)
         w2_q = quantize(w2_bf[:].rearrange("p c j -> p (c j)"), H, "w2")
-        for t in range(PACK):
-            flow_tile(t)
+
+        flow_banks = PASSING + (held_bank(0), held_bank(1))
+        for lead in range(0, PACK, 2):
+            for half in range(HALVES):
+                for t in (lead, lead + 1):
+                    acc = bank(flow_banks[2 * half + t - lead], "flow_acc")
+                    product(acc[:], w1_q, slice(t * P, (t + 1) * P), picked[half], slice(0, HALF))
+                    nc.scalar.activation(
+                        flows[t][:, half * HALF : (half + 1) * HALF], acc[:], ACT.Copy, scale=-PART
+                    )
+
         others = {}
-        for half, t in [(0, 0), (0, 1), (0, 2), (0, 3), (1, 0), (1, 1)]:
-            others[t, half] = keep.tile([P, HALF], F32, name="other%d_%d" % (t, half))
-            fetch(t, half, others[t, half][:])
-            if half == 0:
-                nc.vector.tensor_tensor(posts[0][:, t, :], others[t, 0][:], flows[t][:, :HALF], ALU.add)
 
-        w3_bf = keep.tile([P, N, PACK], BF16, name="w3_bf", align_bytes=64)
-        nc.vector.tensor_copy(
-            w3_bf[:].rearrange("p (c i) j -> p c j i", i=4),
-            w3_raw[:].rearrange("p j (c i) -> p c j i", i=4),
-        )
-
-        w3_q = quantize(w3_bf[:].rearrange("p c j -> p (c j)"), N, "w3")
-        def stage(slot, shape, dtype, name):
-            return keep.tile(shape, dtype, name=name, tag="stage%d" % slot, align_bytes=64)
-
-        PAIRS = BLOCKS // 2
-        squashed = [stage(k + 1, [P, 2, H], F32, "squashed") for k in range(PAIRS)]
-        limit_acc = {}
-        for b in [4, 5, 6, 7, 2, 3, 0, 1]:
-            half, c = divmod(b, HALF // BLOCK)
-            acc = bank(b, "limit_acc")
-            product(acc[:], picked[half], slice(c * BLOCK, (c + 1) * BLOCK), w2_q, slice(0, H))
-            limit_acc[b] = acc[:].rearrange("j (m t) -> j t m", t=PACK)
-            nc.scalar.activation(
-                squashed[b // 2][:, b % 2, :].rearrange("j (t m) -> j t m", t=PACK), limit_acc[b], ACT.Sigmoid
+        def fetch(t, half, tag):
+            others[t, half] = buffer(tag, [P, HALF], F32, "other")
+            nc.vector.tensor_tensor(
+                others[t, half][:], flows[t][:].indirect(entries(outl_t, half)), factors[t, half][:], ALU.mult
             )
+
+        for t, tag in enumerate(("w2_raw", "w_bf", "other2", "other3")):
+            fetch(t, 0, tag)
+            nc.vector.tensor_tensor(drops[0][:, t, :], others[t, 0][:], flows[t][:, :HALF], ALU.add)
+        for t in range(2):
+            fetch(t, 1, "other%d" % t)
+
+        squashed = {pair: buffer("squashed%d" % pair, [P, 2, H], F32, "squashed") for pair in range(1, PAIRS)}
+        squashed_first = [buffer("squashed0", [P, H], F32, "first"), buffer("second", [P, H], F32, "second")]
+        limits = {}
+
+        def limit(block, number):
+            half, place = divmod(block, HALF // BLOCK)
+            acc = bank(number, "limit_acc")
+            product(acc[:], picked[half], slice(place * BLOCK, (place + 1) * BLOCK), w2_q, slice(0, H))
+            limits[block] = acc[:].rearrange("j (m t) -> j t m", t=PACK)
+
+        for block in list(range(2, BLOCKS)) + [0, 1]:
+            limit(block, held_bank(block) if block < HELD else PASSING[block % 2])
+            target = squashed_first[block][:] if block < 2 else squashed[block // 2][:, block % 2, :]
+            nc.scalar.activation(by_tile(target), limits[block], ACT.Sigmoid)
 
         half_unit = keep.tile([P, PACK], F32, name="half_unit")
         nc.vector.tensor_scalar(half_unit[:], unit_t[:], 0.5, None, ALU.mult)
 
-        neg_caps = []
         logs = []
-        for k in range(PAIRS):
-            logged = stage(k, [P, 2, H], F32, "logged")
-            nc.scalar.activation(logged[:], squashed[k][:], ACT.Ln, bias=TINY, scale=math.exp(-0.5))
-            logs.append(logged)
+        neg_caps = []
+        sizes = {}
+        gaps = {}
+        overs = {}
 
-        def neg_cap(b):
-            cap = keep.tile([P, H], F32, name="neg_cap%d" % b)
+        def logarithm(tag, source, shape):
+            logged = buffer(tag, shape, F32, "logged")
+            nc.scalar.activation(logged[:], source[:], ACT.Ln, bias=TINY, scale=math.exp(-0.5))
+            return logged
+
+        def neg_cap(block):
+            cap = keep.tile([P, H], F32, name="neg_cap%d" % block)
             nc.vector.scalar_tensor_tensor(
-                cap[:].rearrange("j (t m) -> j t m", t=PACK),
-                limit_acc[b],
-                -0.5,
-                logs[b // 2][:, b % 2, :].rearrange("j (t m) -> j t m", t=PACK),
-                ALU.add,
-                ALU.min,
+                by_tile(cap[:]), limits[block], -0.5, by_tile(logs[block]), ALU.add, ALU.min
             )
             neg_caps.append(cap)
 
-        def excess(b):
-            half, c = divmod(b, HALF // BLOCK)
-            turned = bank((0, 2, 4)[b % 3], "turned")
-            for t in range(PACK):
-                nc.tensor.transpose(
-                    turned[:, t * P : (t + 1) * P],
-                    posts[half][:, t, c * BLOCK : (c + 1) * BLOCK],
-                    identity[:],
-                )
-            size = ring.tile([P, H], F32, name="size")
-            nc.scalar.activation(size[:], turned[:], ACT.Abs, scale=1.0 / FLOW)
-            gap = bank((1, 3, 5)[b % 3], "gap")
+        def magnitude(block):
+            turned = bank(PASSING[block % 2], "turned")
+            for t in reversed(range(PACK)):
+                nc.tensor.transpose(turned[:, t * P : (t + 1) * P], drop_of(block)[:, t, :], identity[:])
+            sizes[block] = buffer("second" if block == 0 else "size%d" % block, [P, H], F32, "size")
+            nc.scalar.activation(sizes[block][:], turned[:], ACT.Abs, scale=1.0 / PART)
+
+        def relieved(block):
+            return block >= 2 and block % 2 == 0
+
+        def excess(block):
+            gap = bank(held_bank(block), "gap")
             for t in range(PACK):
                 cols = slice(t * P, (t + 1) * P)
-                nc.tensor.matmul(gap[:, cols], size[:, cols], identity[:], start=True, stop=False, is_transpose=True)
-                nc.tensor.matmul(gap[:, cols], neg_caps[b][:, cols], identity[:], start=False, stop=True, is_transpose=True)
-            return gap
+                nc.tensor.matmul(
+                    gap[:, cols], sizes[block][:, cols], identity[:], start=True, stop=False, is_transpose=True
+                )
+                nc.tensor.matmul(
+                    gap[:, cols], neg_caps[block][:, cols], identity[:], start=False, stop=True, is_transpose=True
+                )
+            gaps[block] = gap
+            if relieved(block):
+                overs[block] = keep.tile([P, PACK, BLOCK], F32, name="over%d" % block)
+                nc.scalar.activation(overs[block][:], gap[:].rearrange("p (t j) -> p t j", t=PACK), ACT.Relu)
 
-        def fold(b, e, gap, largest, mixed):
-            half, c = divmod(b, HALF // BLOCK)
+        def fold(block, largest, mixed):
+            place = block % 2
             groups = BLOCK // D
             nc.vector.tensor_reduce(
-                largest[:, :, e * groups : (e + 1) * groups],
-                gap[:].rearrange("p (t v d) -> p t v d", t=PACK, d=D),
+                largest[:, :, place * groups : (place + 1) * groups],
+                gaps[block][:].rearrange("p (t v d) -> p t v d", t=PACK, d=D),
                 mybir.AxisListType.X,
                 ALU.max,
             )
-            nc.vector.scalar_tensor_tensor(
-                mixed[:, :, e * BLOCK : (e + 1) * BLOCK],
-                gap[:].rearrange("p (t j) -> p t j", t=PACK),
-                0.0,
-                posts[half][:, :, c * BLOCK : (c + 1) * BLOCK],
-                ALU.max,
-                ALU.add,
-            )
+            target = mixed[:, :, place * BLOCK : (place + 1) * BLOCK]
+            if relieved(block):
+                nc.gpsimd.tensor_tensor(target, overs[block][:], drop_of(block), ALU.add)
+            else:
+                nc.vector.scalar_tensor_tensor(
+                    target,
+                    gaps[block][:].rearrange("p (t j) -> p t j", t=PACK),
+                    0.0,
+                    drop_of(block),
+                    ALU.max,
+                    ALU.add,
+                )
 
-        def hidden(width, largest, mixed, weave):
-            groups = width // D
+        def shares(largest):
+            groups = PAIR // D
             share = ring.tile([P, PACK, groups], F32, name="share")
             nc.vector.scalar_tensor_tensor(
-                share[:], largest[:], 0.0,
+                share[:],
+                largest[:],
+                0.0,
                 half_unit[:].unsqueeze(2).to_broadcast([P, PACK, groups]),
-                ALU.max, ALU.mult,
+                ALU.max,
+                ALU.mult,
             )
-            hid = ring.tile([P, PACK, width], BF16, name="hid")
+            return share
+
+        def hidden(piece, width, share, mixed, copy):
+            hid = keep.tile([P, PACK, width], BF16, name="hid", tag="hid%d" % piece)
             for t in range(PACK):
                 nc.vector.scalar_tensor_tensor(
                     hid[:, t, :].rearrange("p (v d) -> p v d", d=D),
                     mixed[:, t, :].rearrange("p (v d) -> p v d", d=D),
                     unit_t[:, t : t + 1],
-                    share[:, t, :].unsqueeze(2).to_broadcast([P, groups, D]),
+                    share[:, t, :].unsqueeze(2).to_broadcast([P, width // D, D]),
                     ALU.mult,
                     ALU.add,
                 )
             woven = ring.tile([P, width, PACK], BF16, name="woven", align_bytes=64)
-            weave(
-                woven[:].rearrange("p (c i) t -> p c t i", i=4),
-                hid[:].rearrange("p t (c i) -> p c t i", i=4),
-            )
+            copy(*weave_views(woven[:], hid[:]))
             return woven
 
         out_rows = out.rearrange("(g p) j -> p g j", p=P)
+        out_banks = (held_bank(2), held_bank(3)) + PASSING
 
-        def finish(chunk, first, width, woven):
-            hid_q = quantize(woven[:].rearrange("p j t -> p (j t)"), width, "hid%d" % chunk)
-            acc = bank((6, 7)[chunk % 2], "out_acc")
+        def finish(piece, first, width, woven):
+            hid_q = quantize(woven[:].rearrange("p j t -> p (j t)"), width, "hid%d" % piece)
+            acc = bank(out_banks[piece % len(out_banks)], "out_acc")
             for g in range(N // P):
-                product(acc[:, g * width : (g + 1) * width], w3_q, slice(g * P, (g + 1) * P), hid_q, slice(0, width))
-            result = ring.tile([P, N // P, width], F32, name="result")
-            nc.scalar.copy(result[:], acc[:, : (N // P) * width].rearrange("p (g j) -> p g j", j=width))
+                product(
+                    acc[:, g * width : (g + 1) * width], w3_q, slice(g * P, (g + 1) * P), hid_q, slice(0, width)
+                )
+            tag = "hid%d" % (piece + 1) if width == PAIR else "result%d" % piece
+            result = keep.tile([P, N // P, width], F32, name="result", tag=tag)
+            copy = nc.vector.tensor_copy if piece == PAIRS else nc.scalar.copy
+            copy(result[:], acc[:, : (N // P) * width].rearrange("p (g j) -> p g j", j=width))
             nc.sync.dma_start(out_rows[:, :, first : first + width], result[:])
 
-        for t in (2, 3):
-            neg_cap(2 * t - 4)
-            neg_cap(2 * t - 3)
-            others[t, 1] = stage(t - 2, [P, HALF], F32, "other_late")
-            fetch(t, 1, others[t, 1][:])
-        posts.append(keep.tile([P, PACK, HALF], F32, name="post1", tag="factor3_1"))
+        logs.extend(logarithm("logged%d" % block, squashed_first[block], [P, H])[:] for block in range(2))
+        for pair in range(1, PAIRS):
+            if pair <= 2:
+                magnitude(2 * pair - 2)
+                magnitude(2 * pair - 1)
+            logged = logarithm("squashed%d" % (pair - 1), squashed[pair], [P, 2, H])
+            logs.extend([logged[:, 0, :], logged[:, 1, :]])
+
+        for block in range(HALF // BLOCK):
+            neg_cap(block)
+            excess(block)
+            if block in (1, 2):
+                fetch(block + 1, 1, "logged%d" % (block - 1))
+
+        drops.append(keep.tile([P, PACK, HALF], F32, name="drop1", tag="factor%d_1" % (PACK - 1)))
         for t in range(PACK):
-            nc.gpsimd.tensor_tensor(posts[1][:, t, :], others[t, 1][:], flows[t][:, HALF:], ALU.add)
-        for b in range(4, BLOCKS):
-            neg_cap(b)
-        gaps = {0: excess(0), 1: excess(1)}
+            nc.gpsimd.tensor_tensor(drops[1][:, t, :], others[t, 1][:], flows[t][:, HALF:], ALU.add)
+
+        w3_bf = buffer("squashed%d" % (PAIRS - 1), [P, N, PACK], BF16, "w3_bf")
+        nc.scalar.copy(*weave_views(w3_bf[:], w3_raw[:]))
+        w3_q = quantize(w3_bf[:].rearrange("p c j -> p (c j)"), N, "w3")
+        for block in range(HALF // BLOCK, BLOCKS):
+            magnitude(block)
+
         waiting = None
-        for chunk, blocks in enumerate(CHUNKS):
-            width = len(blocks) * BLOCK
-            largest = ring.tile([P, PACK, width // D], F32, name="largest")
-            mixed = ring.tile([P, PACK, width], F32, name="mixed")
-            for e, b in enumerate(blocks):
-                if b + 2 < BLOCKS:
-                    gaps[b + 2] = excess(b + 2)
-                fold(b, e, gaps[b], largest, mixed)
-            if waiting is not None:
-                finish(*waiting)
-            weave = nc.vector.tensor_copy if chunk == len(CHUNKS) - 1 else nc.scalar.copy
-            waiting = (chunk, blocks[0] * BLOCK, width, hidden(width, largest, mixed, weave))
+        for pair in range(PAIRS):
+            largest = ring.tile([P, PACK, PAIR // D], F32, name="largest")
+            mixed = keep.tile([P, PACK, PAIR], F32, name="mixed")
+            for block in (2 * pair, 2 * pair + 1):
+                fold(block, largest, mixed)
+                if block + HELD < BLOCKS:
+                    limit(block + HELD, held_bank(block + HELD))
+            if pair + 2 < PAIRS:
+                for block in (2 * pair + 4, 2 * pair + 5):
+                    neg_cap(block)
+                    excess(block)
+            share = shares(largest)
+            if pair < PAIRS - 1:
+                made = (pair, pair * PAIR, PAIR, hidden(pair, PAIR, share[:], mixed[:], nc.scalar.copy))
+                if waiting is not None:
+                    finish(*waiting)
+                waiting = made
+
+        for place, copy in enumerate((nc.scalar.copy, nc.vector.tensor_copy)):
+            piece = PAIRS - 1 + place
+            woven = hidden(
+                piece,
+                BLOCK,
+                share[:, :, place * (BLOCK // D) : (place + 1) * (BLOCK // D)],
+                mixed[:, :, place * BLOCK : (place + 1) * BLOCK],
+                copy,
+            )
+            finish(*waiting)
+            waiting = (piece, S - PAIR + place * BLOCK, BLOCK, woven)
         finish(*waiting)

import math
from contextlib import ExitStack

import concourse.mybir as mybir
from concourse.masks import make_identity

K, T, S, D, N, H = 512, 2048, 1024, 4, 256, 512
FLOPS = 2 * K * H * S * 2 + 2 * H * N * S

F32 = mybir.dt.float32
BF16 = mybir.dt.bfloat16
I32 = mybir.dt.int32
U32 = mybir.dt.uint32
U16 = mybir.dt.uint16
U8 = mybir.dt.uint8
FP8X4 = mybir.dt.float8_e4m3fn_x4
ALU = mybir.AluOpType
ACT = mybir.ActivationFunctionType

P = 128
PACK = 4
HALF = 512
BLOCK = 128
PAIR = 2 * BLOCK
HALVES = S // HALF
BLOCKS = S // BLOCK
PAIRS = S // PAIR
LIST_ROW = 16
RUN = 4
PART = 0.3
TINY = 2.0 ** -60

HELD = 6
PASSING = (6, 7)


def held_bank(block):
    return (block + 4) % HELD


def tile_picked_ylopfw_risk_p_kernel(
    tc, x_words, x_scales, w1, w2, lodf, unit, w3, offs, out_l, out
):
    nc = tc.nc
    with ExitStack() as ctx:
        keep = ctx.enter_context(tc.tile_pool(name="keep", bufs=1))
        ring = ctx.enter_context(tc.tile_pool(name="ring", bufs=3))
        psum = ctx.enter_context(tc.psum_pool(name="psum", bufs=1))

        def bank(number, name):
            return psum.tile([P, HALF], F32, name=name, tag="bank%d" % number)

        def buffer(tag, shape, dtype, name):
            return keep.tile(shape, dtype, name=name, tag=tag, align_bytes=64)

        def entries(list_tile, half):
            return list_tile[:, half * (HALF // LIST_ROW) : (half + 1) * (HALF // LIST_ROW)]

        def weave_views(woven, rows):
            return (
                woven.rearrange("p (c i) j -> p c j i", i=RUN),
                rows.rearrange("p j (c i) -> p c j i", i=RUN),
            )

        def quantize(values, width, name):
            codes = keep.tile([P, width], U32, name=name + "_codes", align_bytes=64)
            scales = keep.tile([P, width], U8, name=name + "_scales", align_bytes=64)
            nc.vector.quantize_mx(out=codes[:].bitcast(FP8X4), scales=scales[:], in_=values)
            return codes, scales

        def product(acc, stationary, s_cols, moving, m_cols):
            nc.tensor.matmul_mx(
                out=acc,
                lhsT=stationary[0][:, s_cols].bitcast(FP8X4),
                lhsT_scale=stationary[1][:, s_cols],
                rhs=moving[0][:, m_cols].bitcast(FP8X4),
                rhs_scale=moving[1][:, m_cols],
                start=True,
                stop=True,
            )

        def by_tile(view):
            return view.rearrange("j (t m) -> j t m", t=PACK)

        def drop_of(block):
            half, place = divmod(block, HALF // BLOCK)
            return drops[half][:, :, place * BLOCK : (place + 1) * BLOCK]

        offs_t = keep.tile([P, S // LIST_ROW], U16, name="offs_t")
        nc.sync.dma_start(offs_t[:], offs)
        table_scales = keep.tile([P, T], U8, name="table_scales", align_bytes=64)
        nc.gpsimd.memset(table_scales[:].bitcast(I32), 0)
        for quadrant in range(4):
            nc.sync.dma_start(
                table_scales[32 * quadrant : 32 * quadrant + 4, :].bitcast(I32),
                x_scales[0, 4 * quadrant : 4 * quadrant + 4, :].bitcast(I32),
            )
        w1_rows = w1.rearrange("(p j) c -> p j c", j=PACK)
        w1_raw = []
        outl_t = keep.tile([P, S // LIST_ROW], U16, name="outl_t")
        for side in range(2):
            raw = keep.tile([P, PACK, H // 2], F32, name="w1_raw%d" % side)
            nc.sync.dma_start(raw[:], w1_rows[:, :, side * (H // 2) : (side + 1) * (H // 2)])
            w1_raw.append(raw)
        table_words = keep.tile([P, T], I32, name="table_words", align_bytes=64)
        nc.sync.dma_start(table_words[:], x_words[0].rearrange("p n t -> p (n t)").bitcast(I32))
        nc.sync.dma_start(outl_t[:], out_l)
        w2_raw = buffer("w2_raw", [P, PACK, H], F32, "w2_raw")
        nc.sync.dma_start(w2_raw[:], w2.rearrange("(p j) c -> p j c", j=PACK))
        lodf_rows = lodf.rearrange("(p t) j -> p t j", t=PACK)
        factors = {}
        for half in range(HALVES):
            for t in range(PACK):
                factors[t, half] = keep.tile([P, HALF], F32, name="factor%d_%d" % (t, half))
                nc.sync.dma_start(factors[t, half][:], lodf_rows[:, t, half * HALF : (half + 1) * HALF])
        unit_t = keep.tile([P, PACK], F32, name="unit_t")
        nc.sync.dma_start(unit_t[:], unit.rearrange("(p t) o -> p (t o)", t=PACK))
        w3_raw = keep.tile([P, PACK, N], F32, name="w3_raw")
        nc.sync.dma_start(w3_raw[:], w3.rearrange("(p j) c -> p j c", j=PACK))
        identity = keep.tile([P, P], F32, name="identity")
        make_identity(nc, identity[:])

        warm = keep.tile([P, 1], F32, name="warm")
        nc.scalar.activation(warm[:], identity[:, 0:1], ACT.Sigmoid)

        picked_scales = []
        for half in range(HALVES):
            scales = keep.tile([P, HALF], U8, name="picked_scales%d" % half, align_bytes=64)
            nc.vector.tensor_copy(scales[:], table_scales[:].indirect(entries(offs_t, half)))
            picked_scales.append(scales)
        picked = []
        for half in range(HALVES):
            words = keep.tile([P, HALF], U32, name="picked_words%d" % half, align_bytes=64)
            nc.vector.tensor_copy(words[:], table_words[:].bitcast(U32).indirect(entries(offs_t, half)))
            picked.append((words, picked_scales[half]))

        w1_bf = buffer("w_bf", [P, PACK, P, PACK], BF16, "w1_bf")
        for side in range(2):
            nc.scalar.copy(
                w1_bf[:, :, side * (P // 2) : (side + 1) * (P // 2), :].rearrange("p t m j -> p m t j"),
                w1_raw[side][:].rearrange("p j (m t) -> p m t j", t=PACK),
            )
        w1_q = quantize(w1_bf[:].rearrange("p t m j -> p (t m j)"), H, "w1")

        flows = [keep.tile([P, S], F32, name="flow%d" % t) for t in range(PACK)]
        drops = [keep.tile([P, PACK, HALF], F32, name="drop0")]

        w2_bf = buffer("w_bf", [P, H, PACK], BF16, "w2_bf")
        nc.vector.tensor_scalar(*weave_views(w2_bf[:], w2_raw[:]), -1.0, None, ALU.mult)
        w2_q = quantize(w2_bf[:].rearrange("p c j -> p (c j)"), H, "w2")

        flow_banks = PASSING + (held_bank(0), held_bank(1))
        for lead in range(0, PACK, 2):
            for half in range(HALVES):
                for t in (lead, lead + 1):
                    acc = bank(flow_banks[2 * half + t - lead], "flow_acc")
                    product(acc[:], w1_q, slice(t * P, (t + 1) * P), picked[half], slice(0, HALF))
                    nc.scalar.activation(
                        flows[t][:, half * HALF : (half + 1) * HALF], acc[:], ACT.Copy, scale=-PART
                    )

        others = {}

        def fetch(t, half, tag):
            others[t, half] = buffer(tag, [P, HALF], F32, "other")
            nc.vector.tensor_tensor(
                others[t, half][:], flows[t][:].indirect(entries(outl_t, half)), factors[t, half][:], ALU.mult
            )

        for t, tag in enumerate(("w2_raw", "w_bf", "other2", "other3")):
            fetch(t, 0, tag)
            nc.vector.tensor_tensor(drops[0][:, t, :], others[t, 0][:], flows[t][:, :HALF], ALU.add)
        for t in range(2):
            fetch(t, 1, "other%d" % t)

        squashed = {pair: buffer("squashed%d" % pair, [P, 2, H], F32, "squashed") for pair in range(1, PAIRS)}
        squashed_first = [buffer("squashed0", [P, H], F32, "first"), buffer("second", [P, H], F32, "second")]
        limits = {}

        def limit(block, number):
            half, place = divmod(block, HALF // BLOCK)
            acc = bank(number, "limit_acc")
            product(acc[:], picked[half], slice(place * BLOCK, (place + 1) * BLOCK), w2_q, slice(0, H))
            limits[block] = acc[:].rearrange("j (m t) -> j t m", t=PACK)

        for block in list(range(2, BLOCKS)) + [0, 1]:
            limit(block, held_bank(block) if block < HELD else PASSING[block % 2])
            target = squashed_first[block][:] if block < 2 else squashed[block // 2][:, block % 2, :]
            nc.scalar.activation(by_tile(target), limits[block], ACT.Sigmoid)

        half_unit = keep.tile([P, PACK], F32, name="half_unit")
        nc.vector.tensor_scalar(half_unit[:], unit_t[:], 0.5, None, ALU.mult)

        logs = []
        neg_caps = []
        sizes = {}
        gaps = {}
        overs = {}

        def logarithm(tag, source, shape):
            logged = buffer(tag, shape, F32, "logged")
            nc.scalar.activation(logged[:], source[:], ACT.Ln, bias=TINY, scale=math.exp(-0.5))
            return logged

        def neg_cap(block):
            cap = keep.tile([P, H], F32, name="neg_cap%d" % block)
            nc.vector.scalar_tensor_tensor(
                by_tile(cap[:]), limits[block], -0.5, by_tile(logs[block]), ALU.add, ALU.min
            )
            neg_caps.append(cap)

        def magnitude(block):
            turned = bank(PASSING[block % 2], "turned")
            for t in reversed(range(PACK)):
                nc.tensor.transpose(turned[:, t * P : (t + 1) * P], drop_of(block)[:, t, :], identity[:])
            sizes[block] = buffer("second" if block == 0 else "size%d" % block, [P, H], F32, "size")
            nc.scalar.activation(sizes[block][:], turned[:], ACT.Abs, scale=1.0 / PART)

        def relieved(block):
            return block >= 2 and block % 2 == 0

        def excess(block):
            gap = bank(held_bank(block), "gap")
            for t in range(PACK):
                cols = slice(t * P, (t + 1) * P)
                nc.tensor.matmul(
                    gap[:, cols], sizes[block][:, cols], identity[:], start=True, stop=False, is_transpose=True
                )
                nc.tensor.matmul(
                    gap[:, cols], neg_caps[block][:, cols], identity[:], start=False, stop=True, is_transpose=True
                )
            gaps[block] = gap
            if relieved(block):
                overs[block] = keep.tile([P, PACK, BLOCK], F32, name="over%d" % block)
                nc.scalar.activation(overs[block][:], gap[:].rearrange("p (t j) -> p t j", t=PACK), ACT.Relu)

        def fold(block, largest, mixed):
            place = block % 2
            groups = BLOCK // D
            nc.vector.tensor_reduce(
                largest[:, :, place * groups : (place + 1) * groups],
                gaps[block][:].rearrange("p (t v d) -> p t v d", t=PACK, d=D),
                mybir.AxisListType.X,
                ALU.max,
            )
            target = mixed[:, :, place * BLOCK : (place + 1) * BLOCK]
            if relieved(block):
                nc.gpsimd.tensor_tensor(target, overs[block][:], drop_of(block), ALU.add)
            else:
                nc.vector.scalar_tensor_tensor(
                    target,
                    gaps[block][:].rearrange("p (t j) -> p t j", t=PACK),
                    0.0,
                    drop_of(block),
                    ALU.max,
                    ALU.add,
                )

        def shares(largest):
            groups = PAIR // D
            share = ring.tile([P, PACK, groups], F32, name="share")
            nc.vector.scalar_tensor_tensor(
                share[:],
                largest[:],
                0.0,
                half_unit[:].unsqueeze(2).to_broadcast([P, PACK, groups]),
                ALU.max,
                ALU.mult,
            )
            return share

        def hidden(piece, width, share, mixed, copy):
            hid = keep.tile([P, PACK, width], BF16, name="hid", tag="hid%d" % piece)
            for t in range(PACK):
                nc.vector.scalar_tensor_tensor(
                    hid[:, t, :].rearrange("p (v d) -> p v d", d=D),
                    mixed[:, t, :].rearrange("p (v d) -> p v d", d=D),
                    unit_t[:, t : t + 1],
                    share[:, t, :].unsqueeze(2).to_broadcast([P, width // D, D]),
                    ALU.mult,
                    ALU.add,
                )
            woven = ring.tile([P, width, PACK], BF16, name="woven", align_bytes=64)
            copy(*weave_views(woven[:], hid[:]))
            return woven

        out_rows = out.rearrange("(g p) j -> p g j", p=P)
        out_banks = (held_bank(2), held_bank(3)) + PASSING

        def finish(piece, first, width, woven):
            hid_q = quantize(woven[:].rearrange("p j t -> p (j t)"), width, "hid%d" % piece)
            acc = bank(out_banks[piece % len(out_banks)], "out_acc")
            for g in range(N // P):
                product(
                    acc[:, g * width : (g + 1) * width], w3_q, slice(g * P, (g + 1) * P), hid_q, slice(0, width)
                )
            tag = "hid%d" % (piece + 1) if width == PAIR else "result%d" % piece
            result = keep.tile([P, N // P, width], F32, name="result", tag=tag)
            copy = nc.vector.tensor_copy if piece == PAIRS else nc.scalar.copy
            copy(result[:], acc[:, : (N // P) * width].rearrange("p (g j) -> p g j", j=width))
            nc.sync.dma_start(out_rows[:, :, first : first + width], result[:])

        logs.extend(logarithm("logged%d" % block, squashed_first[block], [P, H])[:] for block in range(2))
        for pair in range(1, PAIRS):
            if pair <= 2:
                magnitude(2 * pair - 2)
                magnitude(2 * pair - 1)
            logged = logarithm("squashed%d" % (pair - 1), squashed[pair], [P, 2, H])
            logs.extend([logged[:, 0, :], logged[:, 1, :]])

        for block in range(HALF // BLOCK):
            neg_cap(block)
            excess(block)
            if block in (1, 2):
                fetch(block + 1, 1, "logged%d" % (block - 1))

        drops.append(keep.tile([P, PACK, HALF], F32, name="drop1", tag="factor%d_1" % (PACK - 1)))
        for t in range(PACK):
            nc.gpsimd.tensor_tensor(drops[1][:, t, :], others[t, 1][:], flows[t][:, HALF:], ALU.add)

        w3_bf = buffer("squashed%d" % (PAIRS - 1), [P, N, PACK], BF16, "w3_bf")
        nc.scalar.copy(*weave_views(w3_bf[:], w3_raw[:]))
        w3_q = quantize(w3_bf[:].rearrange("p c j -> p (c j)"), N, "w3")
        for block in range(HALF // BLOCK, BLOCKS):
            magnitude(block)

        waiting = None
        for pair in range(PAIRS):
            largest = ring.tile([P, PACK, PAIR // D], F32, name="largest")
            mixed = keep.tile([P, PACK, PAIR], F32, name="mixed")
            for block in (2 * pair, 2 * pair + 1):
                fold(block, largest, mixed)
                if block + HELD < BLOCKS:
                    limit(block + HELD, held_bank(block + HELD))
            if pair + 2 < PAIRS:
                for block in (2 * pair + 4, 2 * pair + 5):
                    neg_cap(block)
                    excess(block)
            share = shares(largest)
            if pair < PAIRS - 1:
                made = (pair, pair * PAIR, PAIR, hidden(pair, PAIR, share[:], mixed[:], nc.scalar.copy))
                if waiting is not None:
                    finish(*waiting)
                waiting = made

        for place, copy in enumerate((nc.scalar.copy, nc.vector.tensor_copy)):
            piece = PAIRS - 1 + place
            woven = hidden(
                piece,
                BLOCK,
                share[:, :, place * (BLOCK // D) : (place + 1) * (BLOCK // D)],
                mixed[:, :, place * BLOCK : (place + 1) * BLOCK],
                copy,
            )
            finish(*waiting)
            waiting = (piece, S - PAIR + place * BLOCK, BLOCK, woven)
        finish(*waiting)
